import numpy as np
import ml_dtypes


def mxq(x, axis, fmt="e4m3"):
    dtype, down = {"e4m3": (ml_dtypes.float8_e4m3fn, 7), "e5m2": (ml_dtypes.float8_e5m2, 14)}[fmt]
    v = np.moveaxis(np.asarray(x, np.float32).astype(ml_dtypes.bfloat16).astype(np.float64), axis, -1)
    blocks = v.reshape(v.shape[:-1] + (-1, 32))
    amax = np.abs(blocks).max(-1, keepdims=True)
    byte = np.maximum(np.where(amax > 0, np.frexp(amax)[1] - 1 + 127, 0) - down, 1)
    scale = np.exp2(byte - 127.0)
    codes = (blocks / scale).astype(np.float32).astype(dtype).astype(np.float64)
    return np.moveaxis((codes * scale).reshape(v.shape), -1, axis)


WIDE = False


def mx_kscale(k):
    if not WIDE:
        return np.ones(k)
    levels = np.array([10, -10, 5, -5, 0])
    if k % 512:
        return np.exp2(np.random.permutation(np.resize(levels, k // 32))).repeat(32)
    a = np.empty((k // 512, 16))
    for p in range(k // 512):
        a[p, :8] = np.random.permutation(np.resize(levels, 8))
        for g in range(8):
            far = levels[np.abs(levels - a[p, g]) >= 10]
            a[p, g + 8] = far[np.random.randint(len(far))]
    return np.exp2(a.ravel()).repeat(32)


def f64(x):
    return np.asarray(x).astype(np.float64)


def striped(idx):
    return np.tile(np.asarray(idx).reshape(-1, 16).T, (8, 1)).astype(np.uint16)


def unstriped(offs):
    return offs[:16].T.reshape(-1).astype(np.int64)


E2M1 = np.array([0.0, 0.5, 1.0, 1.5, 2.0, 3.0, 4.0, 6.0, -0.0, -0.5, -1.0, -1.5, -2.0, -3.0, -4.0, -6.0])


def pack_weight(w, fmt):
    k, n = w.shape
    w = f64(np.asarray(w, np.float32).astype(ml_dtypes.bfloat16)).reshape(k // 32, 32, n)
    amax = np.abs(w).max(1)
    if fmt == "e4m3":
        byte = np.frexp(amax)[1] - 1 + 127 - 7
    else:
        mant, ex = np.frexp(amax / 6.0)
        byte = np.where(mant > 0.5, ex, ex - 1) + 127
    byte = np.clip(np.where(amax > 0, byte, 1), 1, 254)
    scaled = (w * np.exp2(127.0 - byte)[:, None, :]).reshape(k, n).astype(np.float32)
    by_word = np.ascontiguousarray(scaled.reshape(k // 512, 128, 4, n).transpose(0, 1, 3, 2))
    if fmt == "e4m3":
        words = by_word.astype(ml_dtypes.float8_e4m3fn).view(np.uint8)
    else:
        c = by_word.astype(ml_dtypes.float4_e2m1fn).view(np.uint8) & 0xF
        words = (c[..., 0::2] | (c[..., 1::2] << 4)).reshape(k // 512, 128, 2 * n)
    return np.ascontiguousarray(words), np.ascontiguousarray(byte.astype(np.uint8).reshape(k // 512, 16, n))


def unpack_weight(words, scales, fmt):
    g, _, n = scales.shape
    words = np.ascontiguousarray(words).reshape(g, 128, n, -1)
    if fmt == "e4m3":
        vals = words.view(ml_dtypes.float8_e4m3fn).astype(np.float64)
    else:
        nib = np.empty((g, 128, n, 4), np.uint8)
        nib[..., 0::2] = words & 0xF
        nib[..., 1::2] = words >> 4
        vals = E2M1[nib]
    vals = vals * np.repeat(np.exp2(scales.astype(np.float64) - 127.0), 8, axis=1)[..., None]
    return vals.transpose(0, 1, 3, 2).reshape(g * 512, n)


def bf(x):
    return np.asarray(x, np.float32).astype(ml_dtypes.bfloat16)


def planes(Y):
    r, m = Y.shape
    b = f64(bf(Y)).reshape(r // 32, 32, m)
    amax = np.abs(b).max(1)
    byte = np.clip(np.where(amax > 0, np.frexp(amax)[1] - 1 + 127 - 7, 1), 1, 254)
    codes = (b * np.exp2(127.0 - byte)[:, None, :]).reshape(r, m).astype(np.float32).astype(ml_dtypes.float8_e4m3fn).view(np.uint8)
    words = codes.reshape(r // 512, 128, 4, m).transpose(0, 1, 3, 2)
    return np.ascontiguousarray(words), np.ascontiguousarray(byte.astype(np.uint8).reshape(r // 512, 16, m))


D, T, I, Q, E, U = 512, 2048, 512, 256, 512, 1024


def setup_inputs():
    n = np.random.standard_normal
    idx = np.random.permutation(T)[:I]
    idx2 = np.random.permutation(U)[:I]
    fd = mx_kscale(D)
    fi = mx_kscale(I)
    ti = np.ones(T)
    ti[idx] = fi
    keysp = pack_weight(n((D, T)) / fd[:, None], "e2m1")
    return {
        "query": (n((D, Q)) * 0.7 / np.sqrt(D) * fd[:, None]).astype(np.float32),
        "query2": (n((D, Q)) * 0.7 / np.sqrt(D) * fd[:, None]).astype(np.float32),
        "keys_words": keysp[0],
        "keys_scales": keysp[1],
        "notes": (n((D, U)) / fd[:, None]).astype(np.float32),
        "os": (np.random.uniform(0.02, 0.08, (1, I)) * fi).astype(np.float32),
        "vals": (n((E, T)) / ti).astype(np.float32),
        "offs": striped(idx),
        "offs2": striped(idx2),
    }


def reference(query, query2, keys_words, keys_scales, notes, os, vals, offs, offs2):
    idx = unstriped(offs)
    idx2 = unstriped(offs2)
    keysu = unpack_weight(keys_words, keys_scales, "e2m1")
    queryq = mxq(f64(query), 0, "e4m3")
    keysidxg = keysu[:, idx]
    query2q = mxq(f64(query2), 0, "e4m3")
    notesidx2q = mxq(f64(notes)[:, idx2], 0, "e4m3")
    s = queryq.T @ keysidxg + query2q.T @ notesidx2q
    w = np.maximum(s, 0.0)
    wo1 = w * f64(os)
    wt1 = wo1.T
    vt1 = f64(vals)[:, idx].T
    vt1q = mxq(vt1, 0, "e4m3")
    wt1q = mxq(wt1, 0, "e4m3")
    o = vt1q.T @ wt1q
    words, scales = planes(o)
    return o, words, scales

from contextlib import ExitStack

import concourse.mybir as mybir
from concourse.masks import make_identity

D, T, I, Q, E, U = 512, 2048, 512, 256, 512, 1024
FLOPS = 2 * Q * I * D * 2 + 2 * E * Q * I

F32 = mybir.dt.float32
BF16 = mybir.dt.bfloat16
I32 = mybir.dt.int32
U32 = mybir.dt.uint32
U16 = mybir.dt.uint16
U8 = mybir.dt.uint8
FP8X4 = mybir.dt.float8_e4m3fn_x4
FP4X4 = mybir.dt.float4_e2m1fn_x4
COPY = mybir.ActivationFunctionType.Copy
MAX = mybir.AluOpType.max
MULT = mybir.AluOpType.mult

P = 128
PACK = 4
HALF = 128
HALVES = Q // HALF
SPLIT = 16
ROW_BYTES = 4 * T


def quantize(nc, codes, scales, grouped):
    nc.vector.quantize_mx(out=codes.bitcast(FP8X4), scales=scales, in_=grouped)


def tile_attend_twosources_read_lean_pl_kernel(
    tc, query, query2, keys_words, keys_scales, notes, factors, vals, offs, offs2, out_0, out_1, out_2
):
    nc = tc.nc
    with ExitStack() as ctx:
        sb = ctx.enter_context(tc.tile_pool(name="sb", bufs=1))
        shared = ctx.enter_context(tc.tile_pool(name="shared", bufs=1))
        psum = ctx.enter_context(tc.psum_pool(name="psum", bufs=1))

        def tile(name, shape, dtype, tag=None):
            return sb.tile(shape, dtype, name=name, tag=tag or name, align_bytes=64)

        def placed(name, shape, dtype, offset):
            return shared.tile(shape, dtype, name=name, align_bytes=64, offset=offset)

        token_list = tile("token_list", [P, I // 16], U16)
        note_list = tile("note_list", [P, I // 16], U16)
        key_words = tile("key_words", [P, T], U16)
        key_scales = tile("key_scales", [P, T], U8)
        note_planes = [tile("note_plane%d" % t, [P, U], F32) for t in range(PACK)]
        query_raw = [tile("query_raw%d" % a, [P, PACK, Q], F32) for a in range(2)]
        slot_factor = tile("slot_factor", [P, PACK], F32)
        val_rows = [placed("val_rows%d" % j, [P, T], F32, j * ROW_BYTES) for j in range(PACK)]
        identity = tile("identity", [P, P], F32)

        nc.vector.memset(key_scales[:].bitcast(I32), 0)
        nc.sync.dma_start(token_list[:], offs)
        nc.sync.dma_start(key_words[:].bitcast(I32), keys_words[0].bitcast(I32))
        nc.sync.dma_start(note_list[:], offs2)
        notes_by_plane = notes.rearrange("(p t) u -> t p u", t=PACK)
        for t in range(PACK):
            nc.sync.dma_start(note_planes[t][:], notes_by_plane[t])
        for quad in range(4):
            nc.scalar.dma_start(
                key_scales[32 * quad : 32 * quad + 4, :].bitcast(I32),
                keys_scales[0, 4 * quad : 4 * quad + 4, :].bitcast(I32),
            )
        for a, source in enumerate((query, query2)):
            nc.sync.dma_start(query_raw[a][:], source.rearrange("(p t) q -> p t q", t=PACK))
        nc.gpsimd.dma_start(slot_factor[:], factors.rearrange("o (p r) -> p (o r)", r=PACK))
        vals_by_place = vals.rearrange("(m j) t -> j m t", j=PACK)
        for j in range(PACK):
            nc.sync.dma_start(val_rows[j][:], vals_by_place[j])
        make_identity(nc, identity[:])

        keys_listed = tile("keys_listed", [P, I], U16)
        keys_dealt = tile("keys_dealt", [P, I], U16)
        key_scales_dealt = tile("key_scales_dealt", [P, I], U8)
        nc.vector.tensor_copy(keys_listed[:], key_words[:].indirect(token_list[:]))
        nc.vector.tensor_copy(
            keys_dealt[:].rearrange("p (r m) -> p r m", r=PACK),
            keys_listed[:].rearrange("p (m r) -> p r m", r=PACK),
        )
        nc.vector.tensor_copy(
            key_scales_dealt[:].rearrange("p (r m) -> p m r", r=PACK),
            key_scales[:].indirect(token_list[:]),
        )

        notes_listed = tile("notes_listed", [P, PACK, I], BF16)
        for t in range(PACK):
            window = note_planes[t][:].indirect(note_list[:])
            if t % 2 == 0:
                nc.scalar.activation(notes_listed[:, t, :], window, COPY)
            else:
                nc.vector.tensor_copy(notes_listed[:, t, :], window)
        notes_grouped = tile("notes_grouped", [P, I * PACK], BF16)
        nc.vector.tensor_copy(
            notes_grouped[:].rearrange("p (r m t) -> p m r t", r=PACK, t=PACK),
            notes_listed[:].rearrange("p t (m r) -> p m r t", r=PACK),
        )
        note_codes = tile("note_codes", [P, I], U32)
        note_scales = tile("note_scales", [P, I], U8)
        quantize(nc, note_codes[:], note_scales[:], notes_grouped[:])

        query_codes, query_scales = [], []
        for a in range(2):
            grouped = tile("query_grouped%d" % a, [P, Q * PACK], BF16)
            nc.scalar.copy(
                grouped[:].rearrange("p (c i t) -> p c t i", i=4, t=PACK),
                query_raw[a][:].rearrange("p t (c i) -> p c t i", i=4),
            )
            query_codes.append(tile("query_codes%d" % a, [P, Q], U32))
            query_scales.append(tile("query_scales%d" % a, [P, Q], U8))
            quantize(nc, query_codes[a][:], query_scales[a][:], grouped[:])

        weight_codes, weight_scales = [], []
        for h in range(HALVES):
            rows = slice(h * HALF, (h + 1) * HALF)
            scores = psum.tile([P, PACK, HALF], F32, name="scores%d" % h, tag="bank%d" % h)
            for r in range(PACK):
                slots = slice(r * P, (r + 1) * P)
                nc.tensor.matmul_mx(
                    out=scores[:, r, :],
                    lhsT=keys_dealt[:, slots].bitcast(FP4X4),
                    lhsT_scale=key_scales_dealt[:, slots],
                    rhs=query_codes[0][:, rows].bitcast(FP8X4),
                    rhs_scale=query_scales[0][:, rows],
                    start=True,
                    stop=False,
                )
                nc.tensor.matmul_mx(
                    out=scores[:, r, :],
                    lhsT=note_codes[:, slots].bitcast(FP8X4),
                    lhsT_scale=note_scales[:, slots],
                    rhs=query_codes[1][:, rows].bitcast(FP8X4),
                    rhs_scale=query_scales[1][:, rows],
                    start=False,
                    stop=True,
                )
            grouped = tile("weights_grouped%d" % h, [P, HALF, PACK], BF16)
            nc.vector.scalar_tensor_tensor(
                grouped[:],
                scores[:].rearrange("p r q -> p q r"),
                0.0,
                slot_factor[:].unsqueeze(1).to_broadcast([P, HALF, PACK]),
                MAX,
                MULT,
            )
            weight_codes.append(tile("weight_codes%d" % h, [P, HALF], U32))
            weight_scales.append(tile("weight_scales%d" % h, [P, HALF], U8))
            quantize(nc, weight_codes[h][:], weight_scales[h][:], grouped[:].rearrange("p q r -> p (q r)"))

        sums = [psum.tile([P, PACK, HALF], F32, name="sums%d" % h) for h in range(HALVES)]
        results = [placed("result0", [P, 2, Q], F32, 3 * ROW_BYTES + 1024), tile("result1", [P, 2, Q], F32)]
        result_grouped = tile("result_grouped", [P, Q, PACK], BF16)
        out_by_place = out_0.rearrange("(m j) q -> m j q", j=PACK)

        def gather_values(j):
            listed = tile("vals_listed%d" % j, [P, I], BF16)
            if j < 2:
                nc.scalar.activation(listed[:], val_rows[j][:].indirect(token_list[:]), COPY)
            else:
                nc.vector.tensor_copy(listed[:, : 16 * SPLIT], val_rows[j][:].indirect(token_list[:, :SPLIT]))
                nc.scalar.activation(listed[:, 16 * SPLIT :], val_rows[j][:].indirect(token_list[:, SPLIT:]), COPY)
            return listed

        def turn_values(j, listed):
            pairs = listed[:].bitcast(F32)
            turned = psum.tile([P, 2, P], F32, name="turned%d" % j, tag="bank%d" % j)
            for u in range(2):
                nc.tensor.transpose(turned[:, u, :], pairs[:, u::2], identity[:])
            if j == 1:
                grouped = placed("vals_grouped1", [P, P * PACK], BF16, 2 * ROW_BYTES)
            else:
                grouped = tile("vals_grouped%d" % j, [P, P * PACK], BF16)
            copy = nc.vector.tensor_copy if j == 0 else nc.scalar.copy
            copy(grouped[:].bitcast(F32).rearrange("p (m u) -> p m u", u=2), turned[:].rearrange("p u m -> p m u"))
            return grouped

        def multiply(j, grouped):
            if j == 2:
                val_codes = placed("val_codes2", [P, P], U32, 3 * ROW_BYTES)
            else:
                val_codes = tile("val_codes%d" % j, [P, P], U32)
            val_scales = tile("val_scales%d" % j, [P, P], U8)
            quantize(nc, val_codes[:], val_scales[:], grouped[:])
            for h in range(HALVES):
                nc.tensor.matmul_mx(
                    out=sums[h][:, j, :],
                    lhsT=val_codes[:].bitcast(FP8X4),
                    lhsT_scale=val_scales[:],
                    rhs=weight_codes[h][:].bitcast(FP8X4),
                    rhs_scale=weight_scales[h][:],
                    start=True,
                    stop=True,
                )

        def copy_results(c):
            nc.vector.tensor_copy(results[c][:, :, :HALF], sums[0][:, 2 * c : 2 * c + 2, :])
            nc.scalar.copy(results[c][:, :, HALF:], sums[1][:, 2 * c : 2 * c + 2, :])

        multiply(0, turn_values(0, gather_values(0)))
        listed1 = gather_values(1)
        listed2 = gather_values(2)
        multiply(1, turn_values(1, listed1))
        grouped2 = turn_values(2, listed2)
        listed3 = gather_values(3)
        grouped3 = turn_values(3, listed3)
        copy_results(0)
        nc.sync.dma_start(out_by_place[:, 0:2, :], results[0][:])
        multiply(2, grouped2)
        multiply(3, grouped3)

        nc.vector.tensor_copy(result_grouped[:, :HALF, :], sums[0][:].rearrange("p j q -> p q j"))
        nc.scalar.copy(result_grouped[:, HALF:, :], sums[1][:].rearrange("p j q -> p q j"))
        copy_results(1)
        result_codes = tile("result_codes", [P, Q], U32)
        result_scales = tile("result_scales", [P, Q], U8)
        quantize(nc, result_codes[:], result_scales[:], result_grouped[:].rearrange("p q j -> p (q j)"))
        nc.scalar.dma_start(out_by_place[:, 2:4, :], results[1][:])
        nc.sync.dma_start(out_1[0].rearrange("p c r -> p (c r)").bitcast(I32), result_codes[:].bitcast(I32))
        for quad in range(4):
            queue = nc.sync if quad < 2 else nc.scalar
            queue.dma_start(
                out_2[0, 4 * quad : 4 * quad + 4, :].bitcast(I32),
                result_scales[32 * quad : 32 * quad + 4, :].bitcast(I32),
            )
